import numpy as np
import ml_dtypes


def mxq(x, axis, fmt="e4m3"):
    dtype, down = {"e4m3": (ml_dtypes.float8_e4m3fn, 7), "e5m2": (ml_dtypes.float8_e5m2, 14)}[fmt]
    v = np.moveaxis(np.asarray(x, np.float32).astype(ml_dtypes.bfloat16).astype(np.float64), axis, -1)
    blocks = v.reshape(v.shape[:-1] + (-1, 32))
    amax = np.abs(blocks).max(-1, keepdims=True)
    byte = np.maximum(np.where(amax > 0, np.frexp(amax)[1] - 1 + 127, 0) - down, 1)
    scale = np.exp2(byte - 127.0)
    codes = (blocks / scale).astype(np.float32).astype(dtype).astype(np.float64)
    return np.moveaxis((codes * scale).reshape(v.shape), -1, axis)


WIDE = False


def mx_kscale(k):
    if not WIDE:
        return np.ones(k)
    levels = np.array([10, -10, 5, -5, 0])
    if k % 512:
        return np.exp2(np.random.permutation(np.resize(levels, k // 32))).repeat(32)
    a = np.empty((k // 512, 16))
    for p in range(k // 512):
        a[p, :8] = np.random.permutation(np.resize(levels, 8))
        for g in range(8):
            far = levels[np.abs(levels - a[p, g]) >= 10]
            a[p, g + 8] = far[np.random.randint(len(far))]
    return np.exp2(a.ravel()).repeat(32)


def f64(x):
    return np.asarray(x).astype(np.float64)


def striped(idx):
    return np.tile(idx.reshape(-1, 16).T, (8, 1)).astype(np.uint16)


def unstriped(offs):
    return offs[:16].T.reshape(-1).astype(np.int64)


E2M1 = np.array([0.0, 0.5, 1.0, 1.5, 2.0, 3.0, 4.0, 6.0, -0.0, -0.5, -1.0, -1.5, -2.0, -3.0, -4.0, -6.0])


def pack_weight(w, fmt):
    k, n = w.shape
    w = f64(np.asarray(w, np.float32).astype(ml_dtypes.bfloat16)).reshape(k // 32, 32, n)
    amax = np.abs(w).max(1)
    if fmt == "e4m3":
        byte = np.frexp(amax)[1] - 1 + 127 - 7
    else:
        mant, ex = np.frexp(amax / 6.0)
        byte = np.where(mant > 0.5, ex, ex - 1) + 127
    byte = np.clip(np.where(amax > 0, byte, 1), 1, 254)
    scaled = (w * np.exp2(127.0 - byte)[:, None, :]).reshape(k, n).astype(np.float32)
    by_word = np.ascontiguousarray(scaled.reshape(k // 512, 128, 4, n).transpose(0, 1, 3, 2))
    if fmt == "e4m3":
        words = by_word.astype(ml_dtypes.float8_e4m3fn).view(np.uint8)
    else:
        c = by_word.astype(ml_dtypes.float4_e2m1fn).view(np.uint8) & 0xF
        words = (c[..., 0::2] | (c[..., 1::2] << 4)).reshape(k // 512, 128, 2 * n)
    return np.ascontiguousarray(words), np.ascontiguousarray(byte.astype(np.uint8).reshape(k // 512, 16, n))


def unpack_weight(words, scales, fmt):
    g, _, n = scales.shape
    words = np.ascontiguousarray(words).reshape(g, 128, n, -1)
    if fmt == "e4m3":
        vals = words.view(ml_dtypes.float8_e4m3fn).astype(np.float64)
    else:
        nib = np.empty((g, 128, n, 4), np.uint8)
        nib[..., 0::2] = words & 0xF
        nib[..., 1::2] = words >> 4
        vals = E2M1[nib]
    vals = vals * np.repeat(np.exp2(scales.astype(np.float64) - 127.0), 8, axis=1)[..., None]
    return vals.transpose(0, 1, 3, 2).reshape(g * 512, n)


def gelu(v):
    return 0.5 * v * (1.0 + np.tanh(np.sqrt(2.0 / np.pi) * (v + 0.044715 * v**3)))


def twice(P):
    return np.random.permutation(np.repeat(np.arange(P), 2))


K, H, T, S, P = 1536, 512, 4096, 1024, 512


def setup_inputs():
    n = np.random.standard_normal
    s = mx_kscale(K)[:, None]
    u = mx_kscale(H)[:, None]
    d = {}
    d["tab_words"], d["tab_scales"] = pack_weight(n((K, T)) * s, "e4m3")
    d["offs"] = striped(np.random.permutation(T)[:S])
    d["pos1"] = striped(np.random.permutation(S)[:P])
    d["pos2"] = striped(np.random.permutation(S)[:P])
    d["pos3"] = striped(twice(P))
    d["w1"] = (1.2 * n((K, H)) / K ** 0.5 / s).astype(np.float32)
    d["w2_words"], d["w2_scales"] = pack_weight(1.8 * n((K, H)) / K ** 0.5 / s, "e4m3")
    d["w3_words"], d["w3_scales"] = pack_weight(n((H, H)) / H ** 0.5 / u, "e2m1")
    d["gain"] = (np.exp(0.3 * n(H)) * u[:, 0]).astype(np.float32)
    d["base"] = (0.6 * n((H, S))).astype(np.float32)
    return d


def reference(tab_words, tab_scales, offs, pos1, pos2, pos3, w1, w2_words, w2_scales,
              w3_words, w3_scales, gain, base):
    v = unpack_weight(tab_words, tab_scales, "e4m3")[:, unstriped(offs)]
    a = mxq(f64(w1), 0, "e4m3").T @ v
    b = unpack_weight(w2_words, w2_scales, "e4m3").T @ v
    h = a + b / (1.0 + np.exp(-b))
    x = (h[:, unstriped(pos1)] - h[:, unstriped(pos2)]) * f64(gain)[:, None]
    y = unpack_weight(w3_words, w3_scales, "e2m1").T @ mxq(x, 0, "e4m3")
    up = y[:, unstriped(pos3)]
    return h * (1.0 / (1.0 + np.exp(-up))) - f64(base)

@@ -1,0 +1,289 @@
+from contextlib import ExitStack
+
+import concourse.mybir as mybir
+
+K, H, T, S, BANDS = 1536, 512, 4096, 1024, 512
+FLOPS = 2 * (2 * K * H * S + H * H * BANDS)
+
+F32 = mybir.dt.float32
+BF16 = mybir.dt.bfloat16
+I32 = mybir.dt.int32
+U32 = mybir.dt.uint32
+U16 = mybir.dt.uint16
+U8 = mybir.dt.uint8
+FP8X4 = mybir.dt.float8_e4m3fn_x4
+FP4X4 = mybir.dt.float4_e2m1fn_x4
+ACT = mybir.ActivationFunctionType
+ALU = mybir.AluOpType
+
+P = 128
+PACK = 4
+PASSES = K // (P * PACK)
+BANK = 512
+HALVES = S // BANK
+SPARE = 16
+PIECES = ((0, 256), (256, 384), (384, 512))
+
+
+def tile_list_groove_defect_bands_kernel(
+    tc, tab_words, tab_scales, offs, pos1, pos2, pos3, w1, w2_words, w2_scales, w3_words, w3_scales, gain, base, out
+):
+    nc = tc.nc
+    with ExitStack() as ctx:
+        lists = ctx.enter_context(tc.tile_pool(name="lists", bufs=1))
+        keep = ctx.enter_context(tc.tile_pool(name="keep", bufs=1))
+        ring = ctx.enter_context(tc.tile_pool(name="ring", bufs=4))
+        psum = ctx.enter_context(tc.psum_pool(name="psum", bufs=1))
+
+        def tile(name, shape, dtype):
+            return keep.tile(shape, dtype, name=name, align_bytes=64)
+
+        def bank(b):
+            return psum.tile([P, BANK], F32, name="bank%d" % b)
+
+        def load_scale_rows(dst, src, passes):
+            for q in range(4):
+                nc.gpsimd.dma_start(
+                    out=dst[32 * q : 32 * q + 4 * passes, :].bitcast(I32),
+                    in_=src[:, 4 * q : 4 * q + 4, :].bitcast(I32),
+                )
+
+        offs_t = lists.tile([P, S // 16], U16, name="offs_t")
+        pos1_t = lists.tile([P, BANDS // 16], U16, name="pos1_t")
+        pos2_t = lists.tile([P, BANDS // 16], U16, name="pos2_t")
+        pos3_t = lists.tile([P, S // 16], U16, name="pos3_t")
+
+        tab_s = tile("tab_s", [P, T], U8)
+        w2_s_raw = tile("w2_s_raw", [P, H], U8)
+        w3_s_raw = tile("w3_s_raw", [P, H], U8)
+        for plane in (tab_s, w2_s_raw, w3_s_raw):
+            nc.vector.memset(plane[:].bitcast(I32), 0)
+        gate = [tile("gate%d" % t, [P, BANDS + SPARE], F32) for t in range(PACK)]
+
+        tab_w = [tile("tab_w%d" % a, [P, T], I32) for a in range(PASSES)]
+        w2_raw = tile("w2_raw", [P, PASSES, H], I32)
+        w1_raw = [tile("w1_raw%d" % a, [P, PACK, H], F32) for a in range(PASSES)]
+        w3_raw = tile("w3_raw", [P, 2 * H], U8)
+        gain_t = tile("gain_t", [P, PACK], F32)
+        base_t = tile("base_t", [P, PACK, S], F32)
+
+        def load_tab(a):
+            nc.sync.dma_start(out=tab_w[a][:], in_=tab_words[a].rearrange("p t i -> p (t i)").bitcast(I32))
+
+        for t in range(PACK):
+            nc.vector.memset(gate[t][:, BANDS:], 0.0)
+        load_tab(0)
+        nc.sync.dma_start(offs_t[:], offs)
+        load_scale_rows(tab_s, tab_scales, PASSES)
+        nc.sync.dma_start(out=w2_raw[:], in_=w2_words.rearrange("a p c i -> p a (c i)").bitcast(I32))
+        load_scale_rows(w2_s_raw, w2_scales, PASSES)
+        load_scale_rows(w3_s_raw, w3_scales, 1)
+        nc.sync.dma_start(out=w3_raw[:].bitcast(I32), in_=w3_words[0].bitcast(I32))
+        load_tab(1)
+        load_tab(2)
+        for a in range(PASSES):
+            nc.sync.dma_start(
+                out=w1_raw[a][:], in_=w1[a * P * PACK : (a + 1) * P * PACK, :].rearrange("(p j) c -> p j c", j=PACK)
+            )
+        nc.sync.dma_start(pos2_t[:], pos2)
+        nc.sync.dma_start(pos1_t[:], pos1)
+        nc.sync.dma_start(out=gain_t[:], in_=gain.rearrange("(p t) -> p t", t=PACK))
+        nc.sync.dma_start(pos3_t[:], pos3)
+        nc.sync.dma_start(out=base_t[:], in_=base.rearrange("(p t) j -> p t j", t=PACK))
+
+        v_s = tile("v_s", [P, S], U8)
+        v_w = [tile("v_w%d" % a, [P, S], U32) for a in range(PASSES)]
+        w2_w = tile("w2_w", [P, PASSES, H], I32)
+        w2_s = tile("w2_s", [P, H], U8)
+
+        def gather_words(a, pieces):
+            n = S // pieces
+            for i in range(pieces):
+                nc.vector.tensor_copy(
+                    v_w[a][:, i * n : (i + 1) * n],
+                    tab_w[a][:].bitcast(U32).indirect(offs_t[:, i * n // 16 : (i + 1) * n // 16]),
+                )
+
+        gather_words(0, 1)
+        nc.vector.tensor_copy(v_s[:], tab_s[:].indirect(offs_t[:]))
+        nc.vector.tensor_copy(
+            w2_w[:].rearrange("p a (t m) -> p a m t", t=PACK), w2_raw[:].rearrange("p a (m t) -> p a m t", t=PACK)
+        )
+        nc.vector.tensor_copy(
+            w2_s[:].rearrange("p (t m) -> p t m", t=PACK), w2_s_raw[:].rearrange("p (m t) -> p t m", t=PACK)
+        )
+
+        w3_w = tile("w3_w", [P, 2 * H], U8)
+        w3_s = tile("w3_s", [P, H], U8)
+        nc.vector.tensor_copy(
+            w3_w[:].rearrange("p (t m b) -> p t m b", t=PACK, b=2),
+            w3_raw[:].rearrange("p (m t b) -> p t m b", t=PACK, b=2),
+        )
+        nc.vector.tensor_copy(
+            w3_s[:].rearrange("p (t m) -> p t m", t=PACK), w3_s_raw[:].rearrange("p (m t) -> p t m", t=PACK)
+        )
+
+        def product_pass(acc, w_words, w_scale, k0, a, t, half, order=(0, 1, 2)):
+            rows = slice(t * P, (t + 1) * P)
+            cols = slice(half * BANK, (half + 1) * BANK)
+            nc.tensor.matmul_mx(
+                out=acc[:],
+                lhsT=w_words[:, rows].bitcast(FP8X4),
+                lhsT_scale=w_scale[k0:P, rows],
+                rhs=v_w[a][:, cols].bitcast(FP8X4),
+                rhs_scale=v_s[4 * a : P, cols],
+                start=(a == order[0]),
+                stop=(a == order[-1]),
+            )
+
+        b_acc = [[bank(HALVES * t + half) for half in range(HALVES)] for t in range(PACK)]
+        h = [tile("h%d" % t, [P, S], F32) for t in range(PACK)]
+        silu_b = [tile("silu_b%d" % t, [P, S], F32) for t in range(PACK)]
+        for a in range(PASSES):
+            if a > 0:
+                gather_words(a, HALVES if a == PASSES - 1 else 1)
+            for t in range(PACK):
+                for half in range(HALVES):
+                    product_pass(b_acc[t][half], w2_w[:, a, :], w2_s, 4 * a, a, t, half)
+        for t in range(PACK):
+            for half in range(HALVES):
+                nc.scalar.activation(
+                    silu_b[t][:, half * BANK : (half + 1) * BANK], b_acc[t][half][:], ACT.Silu
+                )
+
+        w1_w = [tile("w1_w%d" % a, [P, H], U32) for a in range(PASSES)]
+        w1_s = [tile("w1_s%d" % a, [P, H], U8) for a in range(PASSES)]
+        w1_all = tile("tab_w%d" % (PASSES - 1), [P, PASSES * H * PACK], BF16)
+        w1_b = [w1_all[:, a * H * PACK : (a + 1) * H * PACK] for a in range(PASSES)]
+        a_acc = [[bank(HALVES * t + half) for half in range(HALVES)] for t in range(PACK)]
+        def dealt(a, t0, t1):
+            dst = w1_b[a].rearrange("p (t m j) -> p m j t", t=PACK, j=PACK)[:, :, :, t0:t1]
+            src = w1_raw[a][:].rearrange("p j (m t) -> p m j t", t=PACK)[:, :, :, t0:t1]
+            return dst, src
+
+        def quantise_w1(a, t0, t1):
+            nc.vector.quantize_mx(
+                out=w1_w[a][:, t0 * P : t1 * P].bitcast(FP8X4),
+                scales=w1_s[a][:, t0 * P : t1 * P],
+                in_=w1_b[a][:, t0 * P * PACK : t1 * P * PACK],
+            )
+
+        for a in range(PASSES - 1):
+            nc.vector.tensor_copy(*dealt(a, 0, PACK))
+            quantise_w1(a, 0, PACK)
+        last = PASSES - 1
+        nc.vector.tensor_copy(*dealt(last, 0, 1))
+        quantise_w1(last, 0, 1)
+        nc.scalar.copy(*dealt(last, 1, 2))
+        nc.scalar.copy(*dealt(last, 2, 4))
+
+        def product_a(t):
+            order = (0, 1, 2) if t < 2 else (0, 2, 1)
+            for a in order:
+                for half in range(HALVES):
+                    product_pass(a_acc[t][half], w1_w[a], w1_s[a], 0, a, t, half, order)
+
+        def make_h(t):
+            for half in range(HALVES):
+                cols = slice(half * BANK, (half + 1) * BANK)
+                nc.vector.tensor_tensor(h[t][:, cols], a_acc[t][half][:], silu_b[t][:, cols], ALU.add)
+
+        x_b = [tile("x_b%d" % i, [P, m1 - m0, PACK], BF16) for i, (m0, m1) in enumerate(PIECES)]
+        outer = [tile("outer%d" % t, [P, BANDS], F32) for t in range(PACK)]
+        diff = [tile("diff%d" % t, [P, BANDS], F32) for t in range(PACK)]
+
+        def pick_outer(t, m0, m1):
+            nc.vector.tensor_copy(outer[t][:, m0:m1], h[t][:].indirect(pos2_t[:, m0 // 16 : m1 // 16]))
+
+        def pick_inner(t, m0, m1):
+            nc.vector.tensor_tensor(
+                diff[t][:, m0:m1], h[t][:].indirect(pos1_t[:, m0 // 16 : m1 // 16]), outer[t][:, m0:m1], ALU.subtract
+            )
+
+        def round_x(t, i):
+            m0, m1 = PIECES[i]
+            nc.scalar.activation(x_b[i][:, :, t], diff[t][:, m0:m1], ACT.Copy, scale=gain_t[:, t : t + 1])
+
+        product_a(0)
+        make_h(0)
+        quantise_w1(last, 1, 2)
+        product_a(1)
+        for t in range(PACK - 1):
+            pick_outer(t, 0, BANDS)
+            if t == 0:
+                quantise_w1(last, 2, 4)
+                product_a(2)
+                product_a(3)
+            make_h(t + 1)
+            pick_inner(t, 0, BANDS)
+            for i in range(len(PIECES)):
+                round_x(t, i)
+
+        x_w = tile("x_w", [P, BANDS], U32)
+        x_s = tile("x_s", [P, BANDS], U8)
+
+        def quantise_x(i):
+            m0, m1 = PIECES[i]
+            nc.vector.quantize_mx(
+                out=x_w[:, m0:m1].bitcast(FP8X4), scales=x_s[:, m0:m1], in_=x_b[i][:].rearrange("p m t -> p (m t)")
+            )
+
+        t = PACK - 1
+        pick_outer(t, *PIECES[0])
+        for i in range(len(PIECES)):
+            if i + 1 < len(PIECES):
+                pick_outer(t, *PIECES[i + 1])
+            pick_inner(t, *PIECES[i])
+            round_x(t, i)
+        for i in range(len(PIECES)):
+            quantise_x(i)
+
+        def product_y(acc, t, m0, m1):
+            nc.tensor.matmul_mx(
+                out=acc[:, m0:m1],
+                lhsT=w3_w[:, 2 * t * P : 2 * (t + 1) * P].bitcast(FP4X4),
+                lhsT_scale=w3_s[:, t * P : (t + 1) * P],
+                rhs=x_w[:, m0:m1].bitcast(FP8X4),
+                rhs_scale=x_s[:, m0:m1],
+                start=True,
+                stop=True,
+            )
+
+        def make_gate(t, acc, m0, m1, scratch):
+            nc.scalar.activation(scratch, acc[:, m0:m1], ACT.Tanh, scale=0.5)
+            nc.scalar.activation(gate[t][:, m0:m1], scratch, ACT.Copy, scale=0.5, bias=0.5)
+
+        cut = PIECES[-1][0]
+        early, late = bank(0), bank(PACK)
+        for m0, m1 in PIECES[:-1]:
+            product_y(early, 0, m0, m1)
+        product_y(late, 0, cut, BANDS)
+        make_gate(0, early, 0, cut, diff[PACK - 1][:, BANDS - cut :])
+        make_gate(0, late, cut, BANDS, diff[PACK - 1][:, : BANDS - cut])
+        for t in range(1, PACK):
+            acc = bank(t)
+            product_y(acc, t, 0, BANDS)
+            make_gate(t, acc, 0, BANDS, outer[t][:])
+
+        out_v = out.rearrange("(p t) j -> p t j", t=PACK)
+        chunks = [(t, j0, j0 + BANK) for t in range(PACK) for j0 in range(0, S, BANK)]
+        t, j0, j1 = chunks.pop()
+        chunks.extend([(t, j0, (j0 + j1) // 2), (t, (j0 + j1) // 2, j1)])
+
+        def gated(t, j0, j1):
+            prod = ring.tile([P, j1 - j0], F32, name="prod")
+            nc.vector.tensor_tensor(
+                prod[:], gate[t][:].indirect(pos3_t[:, j0 // 16 : j1 // 16]), h[t][:, j0:j1], ALU.mult
+            )
+            return prod
+
+        def finish(prod, t, j0, j1):
+            res = ring.tile([P, j1 - j0], F32, name="res")
+            nc.vector.tensor_tensor(res[:], prod[:], base_t[:, t, j0:j1], ALU.subtract)
+            nc.sync.dma_start(out=out_v[:, t, j0:j1], in_=res[:])
+
+        prod = gated(*chunks[0])
+        for c, chunk in enumerate(chunks):
+            following = gated(*chunks[c + 1]) if c + 1 < len(chunks) else None
+            finish(prod, *chunk)
+            prod = following

@@ -41,9 +41,9 @@ def tile_list_groove_defect_bands_kernel(
         def bank(b):
             return psum.tile([P, BANK], F32, name="bank%d" % b)
 
-        def load_scale_rows(dst, src, passes):
+        def load_scale_rows(queue, dst, src, passes):
             for q in range(4):
-                nc.gpsimd.dma_start(
+                queue.dma_start(
                     out=dst[32 * q : 32 * q + 4 * passes, :].bitcast(I32),
                     in_=src[:, 4 * q : 4 * q + 4, :].bitcast(I32),
                 )
@@ -74,12 +74,10 @@ def tile_list_groove_defect_bands_kernel(
             nc.vector.memset(gate[t][:, BANDS:], 0.0)
         load_tab(0)
         nc.sync.dma_start(offs_t[:], offs)
-        load_scale_rows(tab_s, tab_scales, PASSES)
+        load_scale_rows(nc.sync, tab_s, tab_scales, PASSES)
         nc.sync.dma_start(out=w2_raw[:], in_=w2_words.rearrange("a p c i -> p a (c i)").bitcast(I32))
-        load_scale_rows(w2_s_raw, w2_scales, PASSES)
-        load_scale_rows(w3_s_raw, w3_scales, 1)
-        nc.sync.dma_start(out=w3_raw[:].bitcast(I32), in_=w3_words[0].bitcast(I32))
         load_tab(1)
+        load_scale_rows(nc.sync, w2_s_raw, w2_scales, PASSES)
         load_tab(2)
         for a in range(PASSES):
             nc.sync.dma_start(
@@ -88,6 +86,8 @@ def tile_list_groove_defect_bands_kernel(
         nc.sync.dma_start(pos2_t[:], pos2)
         nc.sync.dma_start(pos1_t[:], pos1)
         nc.sync.dma_start(out=gain_t[:], in_=gain.rearrange("(p t) -> p t", t=PACK))
+        nc.sync.dma_start(out=w3_raw[:].bitcast(I32), in_=w3_words[0].bitcast(I32))
+        load_scale_rows(nc.sync, w3_s_raw, w3_scales, 1)
         nc.sync.dma_start(pos3_t[:], pos3)
         nc.sync.dma_start(out=base_t[:], in_=base.rearrange("(p t) j -> p t j", t=PACK))
 
@@ -111,16 +111,6 @@ def tile_list_groove_defect_bands_kernel(
         )
         nc.vector.tensor_copy(
             w2_s[:].rearrange("p (t m) -> p t m", t=PACK), w2_s_raw[:].rearrange("p (m t) -> p t m", t=PACK)
-        )
-
-        w3_w = tile("w3_w", [P, 2 * H], U8)
-        w3_s = tile("w3_s", [P, H], U8)
-        nc.vector.tensor_copy(
-            w3_w[:].rearrange("p (t m b) -> p t m b", t=PACK, b=2),
-            w3_raw[:].rearrange("p (m t b) -> p t m b", t=PACK, b=2),
-        )
-        nc.vector.tensor_copy(
-            w3_s[:].rearrange("p (t m) -> p t m", t=PACK), w3_s_raw[:].rearrange("p (m t) -> p t m", t=PACK)
         )
 
         def product_pass(acc, w_words, w_scale, k0, a, t, half, order=(0, 1, 2)):
@@ -172,8 +162,13 @@ def tile_list_groove_defect_bands_kernel(
             nc.vector.tensor_copy(*dealt(a, 0, PACK))
             quantise_w1(a, 0, PACK)
         last = PASSES - 1
-        nc.vector.tensor_copy(*dealt(last, 0, 1))
-        quantise_w1(last, 0, 1)
+        first_b = tile("first_b", [P, P, PACK], BF16)
+        nc.vector.tensor_copy(first_b[:], w1_raw[last][:].rearrange("p j (m t) -> p m j t", t=PACK)[:, :, :, 0])
+        nc.vector.quantize_mx(
+            out=w1_w[last][:, 0:P].bitcast(FP8X4),
+            scales=w1_s[last][:, 0:P],
+            in_=first_b[:].rearrange("p m j -> p (m j)"),
+        )
         nc.scalar.copy(*dealt(last, 1, 2))
         nc.scalar.copy(*dealt(last, 2, 4))
 
@@ -205,6 +200,16 @@ def tile_list_groove_defect_bands_kernel(
             nc.scalar.activation(x_b[i][:, :, t], diff[t][:, m0:m1], ACT.Copy, scale=gain_t[:, t : t + 1])
 
         product_a(0)
+        w3_dealt = tile("first_b", [P, 3 * H], U8)
+        w3_w, w3_s = w3_dealt[:, : 2 * H], w3_dealt[:, 2 * H :]
+        nc.vector.tensor_copy(
+            w3_w.bitcast(U16).rearrange("p (t m) -> p m t", t=PACK),
+            w3_raw[:].bitcast(U16).rearrange("p (m t) -> p m t", t=PACK),
+        )
+        nc.vector.tensor_copy(
+            w3_s.rearrange("p (t m) -> p t m", t=PACK), w3_s_raw[:].rearrange("p (m t) -> p t m", t=PACK)
+        )
+
         make_h(0)
         quantise_w1(last, 1, 2)
         product_a(1)
@@ -251,7 +256,10 @@ def tile_list_groove_defect_bands_kernel(
 
         def make_gate(t, acc, m0, m1, scratch):
             nc.scalar.activation(scratch, acc[:, m0:m1], ACT.Tanh, scale=0.5)
-            nc.scalar.activation(gate[t][:, m0:m1], scratch, ACT.Copy, scale=0.5, bias=0.5)
+            if t == 0:
+                nc.vector.tensor_scalar(gate[t][:, m0:m1], scratch, 0.5, 0.5, ALU.mult, ALU.add)
+            else:
+                nc.scalar.activation(gate[t][:, m0:m1], scratch, ACT.Copy, scale=0.5, bias=0.5)
 
         cut = PIECES[-1][0]
         early, late = bank(0), bank(PACK)
@@ -263,7 +271,7 @@ def tile_list_groove_defect_bands_kernel(
         for t in range(1, PACK):
             acc = bank(t)
             product_y(acc, t, 0, BANDS)
-            make_gate(t, acc, 0, BANDS, outer[t][:])
+            make_gate(t, acc, 0, BANDS, outer[t - 1][:])
 
         out_v = out.rearrange("(p t) j -> p t j", t=PACK)
         chunks = [(t, j0, j0 + BANK) for t in range(PACK) for j0 in range(0, S, BANK)]

@@ -1,6 +1,7 @@
 from contextlib import ExitStack
 
 import concourse.mybir as mybir
+from concourse.masks import make_identity
 
 K, H, T, S, BANDS = 1536, 512, 4096, 1024, 512
 FLOPS = 2 * (2 * K * H * S + H * H * BANDS)
@@ -22,6 +23,7 @@ PASSES = K // (P * PACK)
 BANK = 512
 HALVES = S // BANK
 SPARE = 16
+TURNED_CHUNKS = 5
 PIECES = ((0, 256), (256, 384), (384, 512))
 
 
@@ -32,7 +34,7 @@ def tile_list_groove_defect_bands_kernel(
     with ExitStack() as ctx:
         lists = ctx.enter_context(tc.tile_pool(name="lists", bufs=1))
         keep = ctx.enter_context(tc.tile_pool(name="keep", bufs=1))
-        ring = ctx.enter_context(tc.tile_pool(name="ring", bufs=4))
+        ring = ctx.enter_context(tc.tile_pool(name="ring", bufs=9))
         psum = ctx.enter_context(tc.psum_pool(name="psum", bufs=1))
 
         def tile(name, shape, dtype):
@@ -65,39 +67,46 @@ def tile_list_groove_defect_bands_kernel(
         w1_raw = [tile("w1_raw%d" % a, [P, PACK, H], F32) for a in range(PASSES)]
         w3_raw = tile("w3_raw", [P, 2 * H], U8)
         gain_t = tile("gain_t", [P, PACK], F32)
-        base_t = tile("base_t", [P, PACK, S], F32)
+        base_t = [tile("base_t%d" % t, [P, S], F32) for t in range(PACK)]
 
         def load_tab(a):
             nc.sync.dma_start(out=tab_w[a][:], in_=tab_words[a].rearrange("p t i -> p (t i)").bitcast(I32))
 
         for t in range(PACK):
             nc.vector.memset(gate[t][:, BANDS:], 0.0)
+        def load_w1(a):
+            nc.sync.dma_start(
+                out=w1_raw[a][:], in_=w1[a * P * PACK : (a + 1) * P * PACK, :].rearrange("(p j) c -> p j c", j=PACK)
+            )
+
         load_tab(0)
         nc.sync.dma_start(offs_t[:], offs)
-        load_scale_rows(nc.sync, tab_s, tab_scales, PASSES)
+        load_scale_rows(nc.gpsimd, tab_s, tab_scales, PASSES)
         nc.sync.dma_start(out=w2_raw[:], in_=w2_words.rearrange("a p c i -> p a (c i)").bitcast(I32))
         load_tab(1)
         load_scale_rows(nc.sync, w2_s_raw, w2_scales, PASSES)
         load_tab(2)
-        for a in range(PASSES):
-            nc.sync.dma_start(
-                out=w1_raw[a][:], in_=w1[a * P * PACK : (a + 1) * P * PACK, :].rearrange("(p j) c -> p j c", j=PACK)
-            )
+        load_w1(0)
+        nc.sync.dma_start(out=w3_raw[:].bitcast(I32), in_=w3_words[0].bitcast(I32))
+        load_scale_rows(nc.sync, w3_s_raw, w3_scales, 1)
+        load_w1(1)
+        load_w1(2)
         nc.sync.dma_start(pos2_t[:], pos2)
         nc.sync.dma_start(pos1_t[:], pos1)
         nc.sync.dma_start(out=gain_t[:], in_=gain.rearrange("(p t) -> p t", t=PACK))
-        nc.sync.dma_start(out=w3_raw[:].bitcast(I32), in_=w3_words[0].bitcast(I32))
-        load_scale_rows(nc.sync, w3_s_raw, w3_scales, 1)
+        base_v = base.rearrange("(p t) j -> p t j", t=PACK)
+        for t in range(PACK):
+            nc.sync.dma_start(out=base_t[t][:], in_=base_v[:, t, :])
         nc.sync.dma_start(pos3_t[:], pos3)
-        nc.sync.dma_start(out=base_t[:], in_=base.rearrange("(p t) j -> p t j", t=PACK))
 
         v_s = tile("v_s", [P, S], U8)
-        v_w = [tile("v_w%d" % a, [P, S], U32) for a in range(PASSES)]
+        v_w = {}
         w2_w = tile("w2_w", [P, PASSES, H], I32)
         w2_s = tile("w2_s", [P, H], U8)
 
         def gather_words(a, pieces):
             n = S // pieces
+            v_w[a] = tile("tab_s" if a == 1 else "v_w%d" % a, [P, S], U32)
             for i in range(pieces):
                 nc.vector.tensor_copy(
                     v_w[a][:, i * n : (i + 1) * n],
@@ -224,6 +233,27 @@ def tile_list_groove_defect_bands_kernel(
             for i in range(len(PIECES)):
                 round_x(t, i)
 
+        ident = tile("ident", [P, P], F32)
+        make_identity(nc, ident[:])
+        blocks = [slice(c * P, (c + 1) * P) for c in range(BANK // P)]
+
+        def add_turned(acc, src, first, final):
+            for c, block in enumerate(blocks):
+                nc.tensor.matmul(
+                    acc[:, block], src[:, block], ident[:], is_transpose=True,
+                    start=(first and c == 0), stop=(final and c == len(blocks) - 1),
+                )
+
+        turned = {}
+
+        def open_turned(t, j0):
+            turned[t, j0] = bank(PACK + (HALVES * t + j0 // BANK) % PACK)
+            add_turned(turned[t, j0], base_t[t][:, j0 : j0 + BANK], True, False)
+
+        for t in range(2):
+            for j0 in range(0, S, BANK):
+                open_turned(t, j0)
+
         x_w = tile("x_w", [P, BANDS], U32)
         x_s = tile("x_s", [P, BANDS], U8)
 
@@ -255,21 +285,22 @@ def tile_list_groove_defect_bands_kernel(
             )
 
         def make_gate(t, acc, m0, m1, scratch):
+            sign = -1.0
             nc.scalar.activation(scratch, acc[:, m0:m1], ACT.Tanh, scale=0.5)
             if t == 0:
-                nc.vector.tensor_scalar(gate[t][:, m0:m1], scratch, 0.5, 0.5, ALU.mult, ALU.add)
+                nc.vector.tensor_scalar(gate[t][:, m0:m1], scratch, 0.5 * sign, 0.5 * sign, ALU.mult, ALU.add)
             else:
-                nc.scalar.activation(gate[t][:, m0:m1], scratch, ACT.Copy, scale=0.5, bias=0.5)
+                nc.scalar.activation(gate[t][:, m0:m1], scratch, ACT.Copy, scale=0.5 * sign, bias=0.5 * sign)
 
         cut = PIECES[-1][0]
-        early, late = bank(0), bank(PACK)
+        early, late = bank(0), bank(1)
         for m0, m1 in PIECES[:-1]:
             product_y(early, 0, m0, m1)
         product_y(late, 0, cut, BANDS)
         make_gate(0, early, 0, cut, diff[PACK - 1][:, BANDS - cut :])
         make_gate(0, late, cut, BANDS, diff[PACK - 1][:, : BANDS - cut])
         for t in range(1, PACK):
-            acc = bank(t)
+            acc = bank((t + 1) % PACK)
             product_y(acc, t, 0, BANDS)
             make_gate(t, acc, 0, BANDS, outer[t - 1][:])
 
@@ -286,8 +317,20 @@ def tile_list_groove_defect_bands_kernel(
             return prod
 
         def finish(prod, t, j0, j1):
-            res = ring.tile([P, j1 - j0], F32, name="res")
-            nc.vector.tensor_tensor(res[:], prod[:], base_t[:, t, j0:j1], ALU.subtract)
+            if HALVES * t + j0 // BANK < TURNED_CHUNKS:
+                if (t, j0) not in turned:
+                    open_turned(t, j0)
+                add_turned(turned[t, j0], prod, False, True)
+                flipped = ring.tile([P, BANK], F32, name="flipped")
+                nc.scalar.copy(flipped[:], turned[t, j0][:])
+                back = bank(1 + (HALVES * t + j0 // BANK) % 3)
+                for block in blocks:
+                    nc.tensor.transpose(back[:, block], flipped[:, block], ident[:])
+                res = flipped
+                nc.scalar.activation(res[:], back[:], ACT.Copy, scale=-1.0)
+            else:
+                res = prod
+                nc.vector.scalar_tensor_tensor(res[:], prod[:], -1.0, base_t[t][:, j0:j1], ALU.mult, ALU.subtract)
             nc.sync.dma_start(out=out_v[:, t, j0:j1], in_=res[:])
 
         prod = gated(*chunks[0])

@@ -81,16 +81,16 @@ def tile_list_groove_defect_bands_kernel(
 
         load_tab(0)
         nc.sync.dma_start(offs_t[:], offs)
-        load_scale_rows(nc.gpsimd, tab_s, tab_scales, PASSES)
+        load_scale_rows(nc.sync, tab_s, tab_scales, PASSES)
         nc.sync.dma_start(out=w2_raw[:], in_=w2_words.rearrange("a p c i -> p a (c i)").bitcast(I32))
         load_tab(1)
         load_scale_rows(nc.sync, w2_s_raw, w2_scales, PASSES)
         load_tab(2)
         load_w1(0)
-        nc.sync.dma_start(out=w3_raw[:].bitcast(I32), in_=w3_words[0].bitcast(I32))
-        load_scale_rows(nc.sync, w3_s_raw, w3_scales, 1)
         load_w1(1)
         load_w1(2)
+        nc.sync.dma_start(out=w3_raw[:].bitcast(I32), in_=w3_words[0].bitcast(I32))
+        load_scale_rows(nc.sync, w3_s_raw, w3_scales, 1)
         nc.sync.dma_start(pos2_t[:], pos2)
         nc.sync.dma_start(pos1_t[:], pos1)
         nc.sync.dma_start(out=gain_t[:], in_=gain.rearrange("(p t) -> p t", t=PACK))
@@ -106,7 +106,7 @@ def tile_list_groove_defect_bands_kernel(
 
         def gather_words(a, pieces):
             n = S // pieces
-            v_w[a] = tile("tab_s" if a == 1 else "v_w%d" % a, [P, S], U32)
+            v_w[a] = tile("v_w%d" % a, [P, S], U32)
             for i in range(pieces):
                 nc.vector.tensor_copy(
                     v_w[a][:, i * n : (i + 1) * n],
@@ -247,12 +247,11 @@ def tile_list_groove_defect_bands_kernel(
         turned = {}
 
         def open_turned(t, j0):
-            turned[t, j0] = bank(PACK + (HALVES * t + j0 // BANK) % PACK)
+            turned[t, j0] = bank(PACK + j0 // BANK)
             add_turned(turned[t, j0], base_t[t][:, j0 : j0 + BANK], True, False)
 
-        for t in range(2):
-            for j0 in range(0, S, BANK):
-                open_turned(t, j0)
+        for j0 in range(0, S, BANK):
+            open_turned(0, j0)
 
         x_w = tile("x_w", [P, BANDS], U32)
         x_s = tile("x_s", [P, BANDS], U8)
@@ -299,10 +298,13 @@ def tile_list_groove_defect_bands_kernel(
         product_y(late, 0, cut, BANDS)
         make_gate(0, early, 0, cut, diff[PACK - 1][:, BANDS - cut :])
         make_gate(0, late, cut, BANDS, diff[PACK - 1][:, : BANDS - cut])
-        for t in range(1, PACK):
-            acc = bank((t + 1) % PACK)
+
+        def whole_gate(t):
+            acc = bank(2 + t % 2)
             product_y(acc, t, 0, BANDS)
             make_gate(t, acc, 0, BANDS, outer[t - 1][:])
+
+        whole_gate(1)
 
         out_v = out.rearrange("(p t) j -> p t j", t=PACK)
         chunks = [(t, j0, j0 + BANK) for t in range(PACK) for j0 in range(0, S, BANK)]
@@ -323,18 +325,22 @@ def tile_list_groove_defect_bands_kernel(
                 add_turned(turned[t, j0], prod, False, True)
                 flipped = ring.tile([P, BANK], F32, name="flipped")
                 nc.scalar.copy(flipped[:], turned[t, j0][:])
-                back = bank(1 + (HALVES * t + j0 // BANK) % 3)
+                back = bank(6 + j0 // BANK)
                 for block in blocks:
                     nc.tensor.transpose(back[:, block], flipped[:, block], ident[:])
                 res = flipped
                 nc.scalar.activation(res[:], back[:], ACT.Copy, scale=-1.0)
+                queue = nc.scalar
             else:
                 res = prod
+                queue = nc.sync
                 nc.vector.scalar_tensor_tensor(res[:], prod[:], -1.0, base_t[t][:, j0:j1], ALU.mult, ALU.subtract)
-            nc.sync.dma_start(out=out_v[:, t, j0:j1], in_=res[:])
+            queue.dma_start(out=out_v[:, t, j0:j1], in_=res[:])
 
         prod = gated(*chunks[0])
         for c, chunk in enumerate(chunks):
             following = gated(*chunks[c + 1]) if c + 1 < len(chunks) else None
             finish(prod, *chunk)
+            if c in (0, 2):
+                whole_gate(2 + c // 2)
             prod = following

@@ -20,11 +20,18 @@ ALU = mybir.AluOpType
 P = 128
 PACK = 4
 PASSES = K // (P * PACK)
+LAST = PASSES - 1
 BANK = 512
 HALVES = S // BANK
+QUADRANTS = 4
+PER_COLUMN = 16
 SPARE = 16
-TURNED_CHUNKS = 5
 PIECES = ((0, 256), (256, 384), (384, 512))
+TURNED_CHUNKS = 5
+Y_FIRST_BANKS = (0, 1)
+Y_BANKS = (2, 3)
+TURN_BANKS = (4, 5, 6)
+BACK_BANKS = (7, 1)
 
 
 def tile_list_groove_defect_bands_kernel(
@@ -34,63 +41,65 @@ def tile_list_groove_defect_bands_kernel(
     with ExitStack() as ctx:
         lists = ctx.enter_context(tc.tile_pool(name="lists", bufs=1))
         keep = ctx.enter_context(tc.tile_pool(name="keep", bufs=1))
-        ring = ctx.enter_context(tc.tile_pool(name="ring", bufs=9))
+        ring = ctx.enter_context(tc.tile_pool(name="ring", bufs=PACK * HALVES + 1))
         psum = ctx.enter_context(tc.psum_pool(name="psum", bufs=1))
 
         def tile(name, shape, dtype):
             return keep.tile(shape, dtype, name=name, align_bytes=64)
 
-        def bank(b):
-            return psum.tile([P, BANK], F32, name="bank%d" % b)
+        def bank(number):
+            return psum.tile([P, BANK], F32, name="bank%d" % number)
 
-        def load_scale_rows(queue, dst, src, passes):
-            for q in range(4):
-                queue.dma_start(
-                    out=dst[32 * q : 32 * q + 4 * passes, :].bitcast(I32),
-                    in_=src[:, 4 * q : 4 * q + 4, :].bitcast(I32),
-                )
+        def entries(list_tile, j0, j1):
+            return list_tile[:, j0 // PER_COLUMN : j1 // PER_COLUMN]
 
-        offs_t = lists.tile([P, S // 16], U16, name="offs_t")
-        pos1_t = lists.tile([P, BANDS // 16], U16, name="pos1_t")
-        pos2_t = lists.tile([P, BANDS // 16], U16, name="pos2_t")
-        pos3_t = lists.tile([P, S // 16], U16, name="pos3_t")
+        offs_t = lists.tile([P, S // PER_COLUMN], U16, name="offs_t")
+        pos1_t = lists.tile([P, BANDS // PER_COLUMN], U16, name="pos1_t")
+        pos2_t = lists.tile([P, BANDS // PER_COLUMN], U16, name="pos2_t")
+        pos3_t = lists.tile([P, S // PER_COLUMN], U16, name="pos3_t")
 
         tab_s = tile("tab_s", [P, T], U8)
         w2_s_raw = tile("w2_s_raw", [P, H], U8)
         w3_s_raw = tile("w3_s_raw", [P, H], U8)
-        for plane in (tab_s, w2_s_raw, w3_s_raw):
-            nc.vector.memset(plane[:].bitcast(I32), 0)
+        for scale_tile in (tab_s, w2_s_raw, w3_s_raw):
+            nc.vector.memset(scale_tile[:].bitcast(I32), 0)
         gate = [tile("gate%d" % t, [P, BANDS + SPARE], F32) for t in range(PACK)]
 
-        tab_w = [tile("tab_w%d" % a, [P, T], I32) for a in range(PASSES)]
+        tab_w = [tile("tab_w%d" % g, [P, T], I32) for g in range(PASSES)]
         w2_raw = tile("w2_raw", [P, PASSES, H], I32)
-        w1_raw = [tile("w1_raw%d" % a, [P, PACK, H], F32) for a in range(PASSES)]
+        w1_raw = [tile("w1_raw%d" % g, [P, PACK, H], F32) for g in range(PASSES)]
         w3_raw = tile("w3_raw", [P, 2 * H], U8)
         gain_t = tile("gain_t", [P, PACK], F32)
         base_t = [tile("base_t%d" % t, [P, S], F32) for t in range(PACK)]
-
-        def load_tab(a):
-            nc.sync.dma_start(out=tab_w[a][:], in_=tab_words[a].rearrange("p t i -> p (t i)").bitcast(I32))
-
         for t in range(PACK):
             nc.vector.memset(gate[t][:, BANDS:], 0.0)
-        def load_w1(a):
-            nc.sync.dma_start(
-                out=w1_raw[a][:], in_=w1[a * P * PACK : (a + 1) * P * PACK, :].rearrange("(p j) c -> p j c", j=PACK)
-            )
+
+        def load_scale_rows(dst, src, passes):
+            for q in range(QUADRANTS):
+                nc.sync.dma_start(
+                    out=dst[32 * q : 32 * q + 4 * passes, :].bitcast(I32),
+                    in_=src[:, 4 * q : 4 * q + 4, :].bitcast(I32),
+                )
+
+        def load_tab(g):
+            nc.sync.dma_start(out=tab_w[g][:], in_=tab_words[g].rearrange("p t i -> p (t i)").bitcast(I32))
+
+        def load_w1(g):
+            rows = w1[g * P * PACK : (g + 1) * P * PACK, :]
+            nc.sync.dma_start(out=w1_raw[g][:], in_=rows.rearrange("(p j) c -> p j c", j=PACK))
 
         load_tab(0)
         nc.sync.dma_start(offs_t[:], offs)
-        load_scale_rows(nc.sync, tab_s, tab_scales, PASSES)
+        load_scale_rows(tab_s, tab_scales, PASSES)
         nc.sync.dma_start(out=w2_raw[:], in_=w2_words.rearrange("a p c i -> p a (c i)").bitcast(I32))
         load_tab(1)
-        load_scale_rows(nc.sync, w2_s_raw, w2_scales, PASSES)
-        load_tab(2)
+        load_scale_rows(w2_s_raw, w2_scales, PASSES)
         load_w1(0)
+        load_tab(2)
         load_w1(1)
         load_w1(2)
         nc.sync.dma_start(out=w3_raw[:].bitcast(I32), in_=w3_words[0].bitcast(I32))
-        load_scale_rows(nc.sync, w3_s_raw, w3_scales, 1)
+        load_scale_rows(w3_s_raw, w3_scales, 1)
         nc.sync.dma_start(pos2_t[:], pos2)
         nc.sync.dma_start(pos1_t[:], pos1)
         nc.sync.dma_start(out=gain_t[:], in_=gain.rearrange("(p t) -> p t", t=PACK))
@@ -104,88 +113,98 @@ def tile_list_groove_defect_bands_kernel(
         w2_w = tile("w2_w", [P, PASSES, H], I32)
         w2_s = tile("w2_s", [P, H], U8)
 
-        def gather_words(a, pieces):
-            n = S // pieces
-            v_w[a] = tile("v_w%d" % a, [P, S], U32)
-            for i in range(pieces):
+        def gather_words(g, cuts):
+            n = S // cuts
+            v_w[g] = tile("v_w%d" % g, [P, S], U32)
+            for j0 in range(0, S, n):
                 nc.vector.tensor_copy(
-                    v_w[a][:, i * n : (i + 1) * n],
-                    tab_w[a][:].bitcast(U32).indirect(offs_t[:, i * n // 16 : (i + 1) * n // 16]),
+                    v_w[g][:, j0 : j0 + n], tab_w[g][:].bitcast(U32).indirect(entries(offs_t, j0, j0 + n))
                 )
+
+        def deal_scales(dst, src):
+            nc.vector.tensor_copy(dst.rearrange("p (t m) -> p t m", t=PACK), src.rearrange("p (m t) -> p t m", t=PACK))
 
         gather_words(0, 1)
         nc.vector.tensor_copy(v_s[:], tab_s[:].indirect(offs_t[:]))
         nc.vector.tensor_copy(
             w2_w[:].rearrange("p a (t m) -> p a m t", t=PACK), w2_raw[:].rearrange("p a (m t) -> p a m t", t=PACK)
         )
-        nc.vector.tensor_copy(
-            w2_s[:].rearrange("p (t m) -> p t m", t=PACK), w2_s_raw[:].rearrange("p (m t) -> p t m", t=PACK)
-        )
+        deal_scales(w2_s[:], w2_s_raw[:])
 
-        def product_pass(acc, w_words, w_scale, k0, a, t, half, order=(0, 1, 2)):
+        def table_pass(acc, words, scales, g, t, half, order):
             rows = slice(t * P, (t + 1) * P)
             cols = slice(half * BANK, (half + 1) * BANK)
             nc.tensor.matmul_mx(
                 out=acc[:],
-                lhsT=w_words[:, rows].bitcast(FP8X4),
-                lhsT_scale=w_scale[k0:P, rows],
-                rhs=v_w[a][:, cols].bitcast(FP8X4),
-                rhs_scale=v_s[4 * a : P, cols],
-                start=(a == order[0]),
-                stop=(a == order[-1]),
+                lhsT=words[:, rows].bitcast(FP8X4),
+                lhsT_scale=scales[:, rows],
+                rhs=v_w[g][:, cols].bitcast(FP8X4),
+                rhs_scale=v_s[4 * g : P, cols],
+                start=(g == order[0]),
+                stop=(g == order[-1]),
             )
 
+        w1_w = [tile("w1_w%d" % g, [P, H], U32) for g in range(PASSES)]
+        w1_s = [tile("w1_s%d" % g, [P, H], U8) for g in range(PASSES)]
+        w1_b = {}
+
+        def w1_source(g):
+            return w1_raw[g][:].rearrange("p j (m t) -> p m j t", t=PACK)
+
+        def w1_views(g, t0, t1):
+            dst = w1_b[g].rearrange("p (t m j) -> p m j t", t=PACK, j=PACK)
+            return dst[:, :, :, t0:t1], w1_source(g)[:, :, :, t0:t1]
+
+        def quantise_w1(g, t0, t1, rounded):
+            nc.vector.quantize_mx(
+                out=w1_w[g][:, t0 * P : t1 * P].bitcast(FP8X4), scales=w1_s[g][:, t0 * P : t1 * P], in_=rounded
+            )
+
+        in_order = tuple(range(PASSES))
         b_acc = [[bank(HALVES * t + half) for half in range(HALVES)] for t in range(PACK)]
         h = [tile("h%d" % t, [P, S], F32) for t in range(PACK)]
-        silu_b = [tile("silu_b%d" % t, [P, S], F32) for t in range(PACK)]
-        for a in range(PASSES):
-            if a > 0:
-                gather_words(a, HALVES if a == PASSES - 1 else 1)
+        for g in in_order:
+            if g == LAST:
+                w1_b[0] = tile("tab_w1", [P, H * PACK], BF16)[:]
+                nc.vector.tensor_copy(*w1_views(0, 0, PACK))
+                quantise_w1(0, 0, PACK, w1_b[0])
+            if g > 0:
+                gather_words(g, HALVES if g == LAST else 1)
             for t in range(PACK):
                 for half in range(HALVES):
-                    product_pass(b_acc[t][half], w2_w[:, a, :], w2_s, 4 * a, a, t, half)
-        for t in range(PACK):
+                    table_pass(b_acc[t][half], w2_w[:, g, :], w2_s[4 * g : P, :], g, t, half, in_order)
+
+        silu_b = {}
+
+        def make_silu(t, dst):
+            silu_b[t] = dst
             for half in range(HALVES):
-                nc.scalar.activation(
-                    silu_b[t][:, half * BANK : (half + 1) * BANK], b_acc[t][half][:], ACT.Silu
-                )
+                nc.scalar.activation(dst[:, half * BANK : (half + 1) * BANK], b_acc[t][half][:], ACT.Silu)
 
-        w1_w = [tile("w1_w%d" % a, [P, H], U32) for a in range(PASSES)]
-        w1_s = [tile("w1_s%d" % a, [P, H], U8) for a in range(PASSES)]
-        w1_all = tile("tab_w%d" % (PASSES - 1), [P, PASSES * H * PACK], BF16)
-        w1_b = [w1_all[:, a * H * PACK : (a + 1) * H * PACK] for a in range(PASSES)]
-        a_acc = [[bank(HALVES * t + half) for half in range(HALVES)] for t in range(PACK)]
-        def dealt(a, t0, t1):
-            dst = w1_b[a].rearrange("p (t m j) -> p m j t", t=PACK, j=PACK)[:, :, :, t0:t1]
-            src = w1_raw[a][:].rearrange("p j (m t) -> p m j t", t=PACK)[:, :, :, t0:t1]
-            return dst, src
+        make_silu(0, tile("silu_b0", [P, S], F32)[:])
+        make_silu(1, tile("silu_b1", [P, S], F32)[:])
 
-        def quantise_w1(a, t0, t1):
-            nc.vector.quantize_mx(
-                out=w1_w[a][:, t0 * P : t1 * P].bitcast(FP8X4),
-                scales=w1_s[a][:, t0 * P : t1 * P],
-                in_=w1_b[a][:, t0 * P * PACK : t1 * P * PACK],
-            )
-
-        for a in range(PASSES - 1):
-            nc.vector.tensor_copy(*dealt(a, 0, PACK))
-            quantise_w1(a, 0, PACK)
-        last = PASSES - 1
+        w1_rest = tile("tab_w2", [P, 2 * H * PACK], BF16)
+        w1_b[1], w1_b[2] = w1_rest[:, : H * PACK], w1_rest[:, H * PACK :]
+        nc.vector.tensor_copy(*w1_views(1, 0, PACK))
+        quantise_w1(1, 0, PACK, w1_b[1])
         first_b = tile("first_b", [P, P, PACK], BF16)
-        nc.vector.tensor_copy(first_b[:], w1_raw[last][:].rearrange("p j (m t) -> p m j t", t=PACK)[:, :, :, 0])
-        nc.vector.quantize_mx(
-            out=w1_w[last][:, 0:P].bitcast(FP8X4),
-            scales=w1_s[last][:, 0:P],
-            in_=first_b[:].rearrange("p m j -> p (m j)"),
-        )
-        nc.scalar.copy(*dealt(last, 1, 2))
-        nc.scalar.copy(*dealt(last, 2, 4))
+        nc.vector.tensor_copy(first_b[:], w1_source(LAST)[:, :, :, 0])
+        quantise_w1(LAST, 0, 1, first_b[:].rearrange("p m j -> p (m j)"))
+        nc.scalar.copy(*w1_views(LAST, 1, 2))
+        nc.scalar.copy(*w1_views(LAST, 2, PACK))
+        silu_late = tile("w1_raw%d" % LAST, [P, 2 * S], F32)
+        make_silu(2, silu_late[:, :S])
+        make_silu(3, silu_late[:, S:])
+
+        a_acc = {}
 
         def product_a(t):
-            order = (0, 1, 2) if t < 2 else (0, 2, 1)
-            for a in order:
+            order = in_order if t < 2 else (0, LAST, 1)
+            a_acc[t] = [bank(HALVES * t + half) for half in range(HALVES)]
+            for g in order:
                 for half in range(HALVES):
-                    product_pass(a_acc[t][half], w1_w[a], w1_s[a], 0, a, t, half, order)
+                    table_pass(a_acc[t][half], w1_w[g], w1_s[g][0:P, :], g, t, half, order)
 
         def make_h(t):
             for half in range(HALVES):
@@ -197,11 +216,11 @@ def tile_list_groove_defect_bands_kernel(
         diff = [tile("diff%d" % t, [P, BANDS], F32) for t in range(PACK)]
 
         def pick_outer(t, m0, m1):
-            nc.vector.tensor_copy(outer[t][:, m0:m1], h[t][:].indirect(pos2_t[:, m0 // 16 : m1 // 16]))
+            nc.vector.tensor_copy(outer[t][:, m0:m1], h[t][:].indirect(entries(pos2_t, m0, m1)))
 
         def pick_inner(t, m0, m1):
             nc.vector.tensor_tensor(
-                diff[t][:, m0:m1], h[t][:].indirect(pos1_t[:, m0 // 16 : m1 // 16]), outer[t][:, m0:m1], ALU.subtract
+                diff[t][:, m0:m1], h[t][:].indirect(entries(pos1_t, m0, m1)), outer[t][:, m0:m1], ALU.subtract
             )
 
         def round_x(t, i):
@@ -215,17 +234,14 @@ def tile_list_groove_defect_bands_kernel(
             w3_w.bitcast(U16).rearrange("p (t m) -> p m t", t=PACK),
             w3_raw[:].bitcast(U16).rearrange("p (m t) -> p m t", t=PACK),
         )
-        nc.vector.tensor_copy(
-            w3_s.rearrange("p (t m) -> p t m", t=PACK), w3_s_raw[:].rearrange("p (m t) -> p t m", t=PACK)
-        )
-
+        deal_scales(w3_s, w3_s_raw[:])
         make_h(0)
-        quantise_w1(last, 1, 2)
+        quantise_w1(LAST, 1, 2, w1_b[LAST][:, P * PACK : 2 * P * PACK])
         product_a(1)
         for t in range(PACK - 1):
             pick_outer(t, 0, BANDS)
             if t == 0:
-                quantise_w1(last, 2, 4)
+                quantise_w1(LAST, 2, PACK, w1_b[LAST][:, 2 * P * PACK :])
                 product_a(2)
                 product_a(3)
             make_h(t + 1)
@@ -236,41 +252,40 @@ def tile_list_groove_defect_bands_kernel(
         ident = tile("ident", [P, P], F32)
         make_identity(nc, ident[:])
         blocks = [slice(c * P, (c + 1) * P) for c in range(BANK // P)]
-
-        def add_turned(acc, src, first, final):
-            for c, block in enumerate(blocks):
-                nc.tensor.matmul(
-                    acc[:, block], src[:, block], ident[:], is_transpose=True,
-                    start=(first and c == 0), stop=(final and c == len(blocks) - 1),
-                )
-
         turned = {}
 
-        def open_turned(t, j0):
-            turned[t, j0] = bank(PACK + j0 // BANK)
-            add_turned(turned[t, j0], base_t[t][:, j0 : j0 + BANK], True, False)
+        def add_turned(acc, src, opens):
+            for c, block in enumerate(blocks):
+                nc.tensor.matmul(
+                    acc[:, block],
+                    src[:, block],
+                    ident[:],
+                    is_transpose=True,
+                    start=(opens and c == 0),
+                    stop=(not opens and c == len(blocks) - 1),
+                )
 
-        for j0 in range(0, S, BANK):
-            open_turned(0, j0)
+        def open_turned(c):
+            t, half = divmod(c, HALVES)
+            turned[c] = bank(TURN_BANKS[c % len(TURN_BANKS)])
+            add_turned(turned[c], base_t[t][:, half * BANK : (half + 1) * BANK], True)
+
+        for c in range(len(TURN_BANKS)):
+            open_turned(c)
 
         x_w = tile("x_w", [P, BANDS], U32)
         x_s = tile("x_s", [P, BANDS], U8)
-
-        def quantise_x(i):
-            m0, m1 = PIECES[i]
+        final = PACK - 1
+        pick_outer(final, *PIECES[0])
+        for i in range(len(PIECES)):
+            if i + 1 < len(PIECES):
+                pick_outer(final, *PIECES[i + 1])
+            pick_inner(final, *PIECES[i])
+            round_x(final, i)
+        for i, (m0, m1) in enumerate(PIECES):
             nc.vector.quantize_mx(
                 out=x_w[:, m0:m1].bitcast(FP8X4), scales=x_s[:, m0:m1], in_=x_b[i][:].rearrange("p m t -> p (m t)")
             )
-
-        t = PACK - 1
-        pick_outer(t, *PIECES[0])
-        for i in range(len(PIECES)):
-            if i + 1 < len(PIECES):
-                pick_outer(t, *PIECES[i + 1])
-            pick_inner(t, *PIECES[i])
-            round_x(t, i)
-        for i in range(len(PIECES)):
-            quantise_x(i)
 
         def product_y(acc, t, m0, m1):
             nc.tensor.matmul_mx(
@@ -284,63 +299,58 @@ def tile_list_groove_defect_bands_kernel(
             )
 
         def make_gate(t, acc, m0, m1, scratch):
-            sign = -1.0
             nc.scalar.activation(scratch, acc[:, m0:m1], ACT.Tanh, scale=0.5)
             if t == 0:
-                nc.vector.tensor_scalar(gate[t][:, m0:m1], scratch, 0.5 * sign, 0.5 * sign, ALU.mult, ALU.add)
+                nc.vector.tensor_scalar(gate[t][:, m0:m1], scratch, -0.5, -0.5, ALU.mult, ALU.add)
             else:
-                nc.scalar.activation(gate[t][:, m0:m1], scratch, ACT.Copy, scale=0.5 * sign, bias=0.5 * sign)
-
-        cut = PIECES[-1][0]
-        early, late = bank(0), bank(1)
-        for m0, m1 in PIECES[:-1]:
-            product_y(early, 0, m0, m1)
-        product_y(late, 0, cut, BANDS)
-        make_gate(0, early, 0, cut, diff[PACK - 1][:, BANDS - cut :])
-        make_gate(0, late, cut, BANDS, diff[PACK - 1][:, : BANDS - cut])
+                nc.scalar.activation(gate[t][:, m0:m1], scratch, ACT.Copy, scale=-0.5, bias=-0.5)
 
         def whole_gate(t):
-            acc = bank(2 + t % 2)
+            acc = bank(Y_BANKS[t % len(Y_BANKS)])
             product_y(acc, t, 0, BANDS)
             make_gate(t, acc, 0, BANDS, outer[t - 1][:])
 
+        cut = PIECES[-1][0]
+        early, late = bank(Y_FIRST_BANKS[0]), bank(Y_FIRST_BANKS[1])
+        for m0, m1 in PIECES[:-1]:
+            product_y(early, 0, m0, m1)
+        product_y(late, 0, cut, BANDS)
+        make_gate(0, early, 0, cut, diff[final][:, BANDS - cut :])
+        make_gate(0, late, cut, BANDS, diff[final][:, : BANDS - cut])
         whole_gate(1)
 
         out_v = out.rearrange("(p t) j -> p t j", t=PACK)
-        chunks = [(t, j0, j0 + BANK) for t in range(PACK) for j0 in range(0, S, BANK)]
-        t, j0, j1 = chunks.pop()
-        chunks.extend([(t, j0, (j0 + j1) // 2), (t, (j0 + j1) // 2, j1)])
+        chunks = [(t, j0, j0 + BANK) for t in range(PACK) for j0 in range(0, S, BANK)][:-1]
+        chunks.extend([(final, S - BANK, S - BANK // 2), (final, S - BANK // 2, S)])
 
         def gated(t, j0, j1):
             prod = ring.tile([P, j1 - j0], F32, name="prod")
-            nc.vector.tensor_tensor(
-                prod[:], gate[t][:].indirect(pos3_t[:, j0 // 16 : j1 // 16]), h[t][:, j0:j1], ALU.mult
-            )
+            nc.vector.tensor_tensor(prod[:], gate[t][:].indirect(entries(pos3_t, j0, j1)), h[t][:, j0:j1], ALU.mult)
             return prod
 
-        def finish(prod, t, j0, j1):
-            if HALVES * t + j0 // BANK < TURNED_CHUNKS:
-                if (t, j0) not in turned:
-                    open_turned(t, j0)
-                add_turned(turned[t, j0], prod, False, True)
-                flipped = ring.tile([P, BANK], F32, name="flipped")
-                nc.scalar.copy(flipped[:], turned[t, j0][:])
-                back = bank(6 + j0 // BANK)
-                for block in blocks:
-                    nc.tensor.transpose(back[:, block], flipped[:, block], ident[:])
-                res = flipped
-                nc.scalar.activation(res[:], back[:], ACT.Copy, scale=-1.0)
-                queue = nc.scalar
-            else:
-                res = prod
-                queue = nc.sync
-                nc.vector.scalar_tensor_tensor(res[:], prod[:], -1.0, base_t[t][:, j0:j1], ALU.mult, ALU.subtract)
-            queue.dma_start(out=out_v[:, t, j0:j1], in_=res[:])
+        def finish_turned(c, prod, dst):
+            if c not in turned:
+                open_turned(c)
+            add_turned(turned[c], prod, False)
+            flipped = ring.tile([P, BANK], F32, name="flipped")
+            nc.scalar.copy(flipped[:], turned[c][:])
+            back = bank(BACK_BANKS[c % len(BACK_BANKS)])
+            for block in blocks:
+                nc.tensor.transpose(back[:, block], flipped[:, block], ident[:])
+            nc.scalar.activation(flipped[:], back[:], ACT.Copy, scale=-1.0)
+            nc.scalar.dma_start(out=dst, in_=flipped[:])
+
+        def finish_plain(prod, base_cols, dst):
+            nc.vector.scalar_tensor_tensor(prod[:], prod[:], -1.0, base_cols, ALU.mult, ALU.subtract)
+            nc.sync.dma_start(out=dst, in_=prod[:])
 
         prod = gated(*chunks[0])
-        for c, chunk in enumerate(chunks):
+        for c, (t, j0, j1) in enumerate(chunks):
             following = gated(*chunks[c + 1]) if c + 1 < len(chunks) else None
-            finish(prod, *chunk)
-            if c in (0, 2):
-                whole_gate(2 + c // 2)
+            if c < TURNED_CHUNKS:
+                finish_turned(c, prod, out_v[:, t, j0:j1])
+            else:
+                finish_plain(prod, base_t[t][:, j0:j1], out_v[:, t, j0:j1])
+            if j0 == 0 and t + 2 < PACK:
+                whole_gate(t + 2)
             prod = following

from contextlib import ExitStack

import concourse.mybir as mybir
from concourse.masks import make_identity

K, H, T, S, BANDS = 1536, 512, 4096, 1024, 512
FLOPS = 2 * (2 * K * H * S + H * H * BANDS)

F32 = mybir.dt.float32
BF16 = mybir.dt.bfloat16
I32 = mybir.dt.int32
U32 = mybir.dt.uint32
U16 = mybir.dt.uint16
U8 = mybir.dt.uint8
FP8X4 = mybir.dt.float8_e4m3fn_x4
FP4X4 = mybir.dt.float4_e2m1fn_x4
ACT = mybir.ActivationFunctionType
ALU = mybir.AluOpType

P = 128
PACK = 4
PASSES = K // (P * PACK)
LAST = PASSES - 1
BANK = 512
HALVES = S // BANK
QUADRANTS = 4
PER_COLUMN = 16
SPARE = 16
PIECES = ((0, 256), (256, 384), (384, 512))
TURNED_CHUNKS = 5
Y_FIRST_BANKS = (0, 1)
Y_BANKS = (2, 3)
TURN_BANKS = (4, 5, 6)
BACK_BANKS = (7, 1)


def tile_list_groove_defect_bands_kernel(
    tc, tab_words, tab_scales, offs, pos1, pos2, pos3, w1, w2_words, w2_scales, w3_words, w3_scales, gain, base, out
):
    nc = tc.nc
    with ExitStack() as ctx:
        lists = ctx.enter_context(tc.tile_pool(name="lists", bufs=1))
        keep = ctx.enter_context(tc.tile_pool(name="keep", bufs=1))
        ring = ctx.enter_context(tc.tile_pool(name="ring", bufs=PACK * HALVES + 1))
        psum = ctx.enter_context(tc.psum_pool(name="psum", bufs=1))

        def tile(name, shape, dtype):
            return keep.tile(shape, dtype, name=name, align_bytes=64)

        def bank(number):
            return psum.tile([P, BANK], F32, name="bank%d" % number)

        def entries(list_tile, j0, j1):
            return list_tile[:, j0 // PER_COLUMN : j1 // PER_COLUMN]

        offs_t = lists.tile([P, S // PER_COLUMN], U16, name="offs_t")
        pos1_t = lists.tile([P, BANDS // PER_COLUMN], U16, name="pos1_t")
        pos2_t = lists.tile([P, BANDS // PER_COLUMN], U16, name="pos2_t")
        pos3_t = lists.tile([P, S // PER_COLUMN], U16, name="pos3_t")

        tab_s = tile("tab_s", [P, T], U8)
        w2_s_raw = tile("w2_s_raw", [P, H], U8)
        w3_s_raw = tile("w3_s_raw", [P, H], U8)
        for scale_tile in (tab_s, w2_s_raw, w3_s_raw):
            nc.vector.memset(scale_tile[:].bitcast(I32), 0)
        gate = [tile("gate%d" % t, [P, BANDS + SPARE], F32) for t in range(PACK)]

        tab_w = [tile("tab_w%d" % g, [P, T], I32) for g in range(PASSES)]
        w2_raw = tile("w2_raw", [P, PASSES, H], I32)
        w1_raw = [tile("w1_raw%d" % g, [P, PACK, H], F32) for g in range(PASSES)]
        w3_raw = tile("w3_raw", [P, 2 * H], U8)
        gain_t = tile("gain_t", [P, PACK], F32)
        base_t = [tile("base_t%d" % t, [P, S], F32) for t in range(PACK)]
        for t in range(PACK):
            nc.vector.memset(gate[t][:, BANDS:], 0.0)

        def load_scale_rows(dst, src, passes):
            for q in range(QUADRANTS):
                nc.sync.dma_start(
                    out=dst[32 * q : 32 * q + 4 * passes, :].bitcast(I32),
                    in_=src[:, 4 * q : 4 * q + 4, :].bitcast(I32),
                )

        def load_tab(g):
            nc.sync.dma_start(out=tab_w[g][:], in_=tab_words[g].rearrange("p t i -> p (t i)").bitcast(I32))

        def load_w1(g):
            rows = w1[g * P * PACK : (g + 1) * P * PACK, :]
            nc.sync.dma_start(out=w1_raw[g][:], in_=rows.rearrange("(p j) c -> p j c", j=PACK))

        load_tab(0)
        nc.sync.dma_start(offs_t[:], offs)
        load_scale_rows(tab_s, tab_scales, PASSES)
        nc.sync.dma_start(out=w2_raw[:], in_=w2_words.rearrange("a p c i -> p a (c i)").bitcast(I32))
        load_tab(1)
        load_scale_rows(w2_s_raw, w2_scales, PASSES)
        load_w1(0)
        load_tab(2)
        load_w1(1)
        load_w1(2)
        nc.sync.dma_start(out=w3_raw[:].bitcast(I32), in_=w3_words[0].bitcast(I32))
        load_scale_rows(w3_s_raw, w3_scales, 1)
        nc.sync.dma_start(pos2_t[:], pos2)
        nc.sync.dma_start(pos1_t[:], pos1)
        nc.sync.dma_start(out=gain_t[:], in_=gain.rearrange("(p t) -> p t", t=PACK))
        base_v = base.rearrange("(p t) j -> p t j", t=PACK)
        for t in range(PACK):
            nc.sync.dma_start(out=base_t[t][:], in_=base_v[:, t, :])
        nc.sync.dma_start(pos3_t[:], pos3)

        v_s = tile("v_s", [P, S], U8)
        v_w = {}
        w2_w = tile("w2_w", [P, PASSES, H], I32)
        w2_s = tile("w2_s", [P, H], U8)

        def gather_words(g, cuts):
            n = S // cuts
            v_w[g] = tile("v_w%d" % g, [P, S], U32)
            for j0 in range(0, S, n):
                nc.vector.tensor_copy(
                    v_w[g][:, j0 : j0 + n], tab_w[g][:].bitcast(U32).indirect(entries(offs_t, j0, j0 + n))
                )

        def deal_scales(dst, src):
            nc.vector.tensor_copy(dst.rearrange("p (t m) -> p t m", t=PACK), src.rearrange("p (m t) -> p t m", t=PACK))

        gather_words(0, 1)
        nc.vector.tensor_copy(v_s[:], tab_s[:].indirect(offs_t[:]))
        nc.vector.tensor_copy(
            w2_w[:].rearrange("p a (t m) -> p a m t", t=PACK), w2_raw[:].rearrange("p a (m t) -> p a m t", t=PACK)
        )
        deal_scales(w2_s[:], w2_s_raw[:])

        def table_pass(acc, words, scales, g, t, half, order):
            rows = slice(t * P, (t + 1) * P)
            cols = slice(half * BANK, (half + 1) * BANK)
            nc.tensor.matmul_mx(
                out=acc[:],
                lhsT=words[:, rows].bitcast(FP8X4),
                lhsT_scale=scales[:, rows],
                rhs=v_w[g][:, cols].bitcast(FP8X4),
                rhs_scale=v_s[4 * g : P, cols],
                start=(g == order[0]),
                stop=(g == order[-1]),
            )

        w1_w = [tile("w1_w%d" % g, [P, H], U32) for g in range(PASSES)]
        w1_s = [tile("w1_s%d" % g, [P, H], U8) for g in range(PASSES)]
        w1_b = {}

        def w1_source(g):
            return w1_raw[g][:].rearrange("p j (m t) -> p m j t", t=PACK)

        def w1_views(g, t0, t1):
            dst = w1_b[g].rearrange("p (t m j) -> p m j t", t=PACK, j=PACK)
            return dst[:, :, :, t0:t1], w1_source(g)[:, :, :, t0:t1]

        def quantise_w1(g, t0, t1, rounded):
            nc.vector.quantize_mx(
                out=w1_w[g][:, t0 * P : t1 * P].bitcast(FP8X4), scales=w1_s[g][:, t0 * P : t1 * P], in_=rounded
            )

        in_order = tuple(range(PASSES))
        b_acc = [[bank(HALVES * t + half) for half in range(HALVES)] for t in range(PACK)]
        h = [tile("h%d" % t, [P, S], F32) for t in range(PACK)]
        for g in in_order:
            if g == LAST:
                w1_b[0] = tile("tab_w1", [P, H * PACK], BF16)[:]
                nc.vector.tensor_copy(*w1_views(0, 0, PACK))
                quantise_w1(0, 0, PACK, w1_b[0])
            if g > 0:
                gather_words(g, HALVES if g == LAST else 1)
            for t in range(PACK):
                for half in range(HALVES):
                    table_pass(b_acc[t][half], w2_w[:, g, :], w2_s[4 * g : P, :], g, t, half, in_order)

        silu_b = {}

        def make_silu(t, dst):
            silu_b[t] = dst
            for half in range(HALVES):
                nc.scalar.activation(dst[:, half * BANK : (half + 1) * BANK], b_acc[t][half][:], ACT.Silu)

        make_silu(0, tile("silu_b0", [P, S], F32)[:])
        make_silu(1, tile("silu_b1", [P, S], F32)[:])

        w1_rest = tile("tab_w2", [P, 2 * H * PACK], BF16)
        w1_b[1], w1_b[2] = w1_rest[:, : H * PACK], w1_rest[:, H * PACK :]
        nc.vector.tensor_copy(*w1_views(1, 0, PACK))
        quantise_w1(1, 0, PACK, w1_b[1])
        first_b = tile("first_b", [P, P, PACK], BF16)
        nc.vector.tensor_copy(first_b[:], w1_source(LAST)[:, :, :, 0])
        quantise_w1(LAST, 0, 1, first_b[:].rearrange("p m j -> p (m j)"))
        nc.scalar.copy(*w1_views(LAST, 1, 2))
        nc.scalar.copy(*w1_views(LAST, 2, PACK))
        silu_late = tile("w1_raw%d" % LAST, [P, 2 * S], F32)
        make_silu(2, silu_late[:, :S])
        make_silu(3, silu_late[:, S:])

        a_acc = {}

        def product_a(t):
            order = in_order if t < 2 else (0, LAST, 1)
            a_acc[t] = [bank(HALVES * t + half) for half in range(HALVES)]
            for g in order:
                for half in range(HALVES):
                    table_pass(a_acc[t][half], w1_w[g], w1_s[g][0:P, :], g, t, half, order)

        def make_h(t):
            for half in range(HALVES):
                cols = slice(half * BANK, (half + 1) * BANK)
                nc.vector.tensor_tensor(h[t][:, cols], a_acc[t][half][:], silu_b[t][:, cols], ALU.add)

        x_b = [tile("x_b%d" % i, [P, m1 - m0, PACK], BF16) for i, (m0, m1) in enumerate(PIECES)]
        outer = [tile("outer%d" % t, [P, BANDS], F32) for t in range(PACK)]
        diff = [tile("diff%d" % t, [P, BANDS], F32) for t in range(PACK)]

        def pick_outer(t, m0, m1):
            nc.vector.tensor_copy(outer[t][:, m0:m1], h[t][:].indirect(entries(pos2_t, m0, m1)))

        def pick_inner(t, m0, m1):
            nc.vector.tensor_tensor(
                diff[t][:, m0:m1], h[t][:].indirect(entries(pos1_t, m0, m1)), outer[t][:, m0:m1], ALU.subtract
            )

        def round_x(t, i):
            m0, m1 = PIECES[i]
            nc.scalar.activation(x_b[i][:, :, t], diff[t][:, m0:m1], ACT.Copy, scale=gain_t[:, t : t + 1])

        product_a(0)
        w3_dealt = tile("first_b", [P, 3 * H], U8)
        w3_w, w3_s = w3_dealt[:, : 2 * H], w3_dealt[:, 2 * H :]
        nc.vector.tensor_copy(
            w3_w.bitcast(U16).rearrange("p (t m) -> p m t", t=PACK),
            w3_raw[:].bitcast(U16).rearrange("p (m t) -> p m t", t=PACK),
        )
        deal_scales(w3_s, w3_s_raw[:])
        make_h(0)
        quantise_w1(LAST, 1, 2, w1_b[LAST][:, P * PACK : 2 * P * PACK])
        product_a(1)
        for t in range(PACK - 1):
            pick_outer(t, 0, BANDS)
            if t == 0:
                quantise_w1(LAST, 2, PACK, w1_b[LAST][:, 2 * P * PACK :])
                product_a(2)
                product_a(3)
            make_h(t + 1)
            pick_inner(t, 0, BANDS)
            for i in range(len(PIECES)):
                round_x(t, i)

        ident = tile("ident", [P, P], F32)
        make_identity(nc, ident[:])
        blocks = [slice(c * P, (c + 1) * P) for c in range(BANK // P)]
        turned = {}

        def add_turned(acc, src, opens):
            for c, block in enumerate(blocks):
                nc.tensor.matmul(
                    acc[:, block],
                    src[:, block],
                    ident[:],
                    is_transpose=True,
                    start=(opens and c == 0),
                    stop=(not opens and c == len(blocks) - 1),
                )

        def open_turned(c):
            t, half = divmod(c, HALVES)
            turned[c] = bank(TURN_BANKS[c % len(TURN_BANKS)])
            add_turned(turned[c], base_t[t][:, half * BANK : (half + 1) * BANK], True)

        for c in range(len(TURN_BANKS)):
            open_turned(c)

        x_w = tile("x_w", [P, BANDS], U32)
        x_s = tile("x_s", [P, BANDS], U8)
        final = PACK - 1
        pick_outer(final, *PIECES[0])
        for i in range(len(PIECES)):
            if i + 1 < len(PIECES):
                pick_outer(final, *PIECES[i + 1])
            pick_inner(final, *PIECES[i])
            round_x(final, i)
        for i, (m0, m1) in enumerate(PIECES):
            nc.vector.quantize_mx(
                out=x_w[:, m0:m1].bitcast(FP8X4), scales=x_s[:, m0:m1], in_=x_b[i][:].rearrange("p m t -> p (m t)")
            )

        def product_y(acc, t, m0, m1):
            nc.tensor.matmul_mx(
                out=acc[:, m0:m1],
                lhsT=w3_w[:, 2 * t * P : 2 * (t + 1) * P].bitcast(FP4X4),
                lhsT_scale=w3_s[:, t * P : (t + 1) * P],
                rhs=x_w[:, m0:m1].bitcast(FP8X4),
                rhs_scale=x_s[:, m0:m1],
                start=True,
                stop=True,
            )

        def make_gate(t, acc, m0, m1, scratch):
            nc.scalar.activation(scratch, acc[:, m0:m1], ACT.Tanh, scale=0.5)
            if t == 0:
                nc.vector.tensor_scalar(gate[t][:, m0:m1], scratch, -0.5, -0.5, ALU.mult, ALU.add)
            else:
                nc.scalar.activation(gate[t][:, m0:m1], scratch, ACT.Copy, scale=-0.5, bias=-0.5)

        def whole_gate(t):
            acc = bank(Y_BANKS[t % len(Y_BANKS)])
            product_y(acc, t, 0, BANDS)
            make_gate(t, acc, 0, BANDS, outer[t - 1][:])

        cut = PIECES[-1][0]
        early, late = bank(Y_FIRST_BANKS[0]), bank(Y_FIRST_BANKS[1])
        for m0, m1 in PIECES[:-1]:
            product_y(early, 0, m0, m1)
        product_y(late, 0, cut, BANDS)
        make_gate(0, early, 0, cut, diff[final][:, BANDS - cut :])
        make_gate(0, late, cut, BANDS, diff[final][:, : BANDS - cut])
        whole_gate(1)

        out_v = out.rearrange("(p t) j -> p t j", t=PACK)
        chunks = [(t, j0, j0 + BANK) for t in range(PACK) for j0 in range(0, S, BANK)][:-1]
        chunks.extend([(final, S - BANK, S - BANK // 2), (final, S - BANK // 2, S)])

        def gated(t, j0, j1):
            prod = ring.tile([P, j1 - j0], F32, name="prod")
            nc.vector.tensor_tensor(prod[:], gate[t][:].indirect(entries(pos3_t, j0, j1)), h[t][:, j0:j1], ALU.mult)
            return prod

        def finish_turned(c, prod, dst):
            if c not in turned:
                open_turned(c)
            add_turned(turned[c], prod, False)
            flipped = ring.tile([P, BANK], F32, name="flipped")
            nc.scalar.copy(flipped[:], turned[c][:])
            back = bank(BACK_BANKS[c % len(BACK_BANKS)])
            for block in blocks:
                nc.tensor.transpose(back[:, block], flipped[:, block], ident[:])
            nc.scalar.activation(flipped[:], back[:], ACT.Copy, scale=-1.0)
            nc.scalar.dma_start(out=dst, in_=flipped[:])

        def finish_plain(prod, base_cols, dst):
            nc.vector.scalar_tensor_tensor(prod[:], prod[:], -1.0, base_cols, ALU.mult, ALU.subtract)
            nc.sync.dma_start(out=dst, in_=prod[:])

        prod = gated(*chunks[0])
        for c, (t, j0, j1) in enumerate(chunks):
            following = gated(*chunks[c + 1]) if c + 1 < len(chunks) else None
            if c < TURNED_CHUNKS:
                finish_turned(c, prod, out_v[:, t, j0:j1])
            else:
                finish_plain(prod, base_t[t][:, j0:j1], out_v[:, t, j0:j1])
            if j0 == 0 and t + 2 < PACK:
                whole_gate(t + 2)
            prod = following
